import numpy as np
import ml_dtypes


def mxq(x, axis, fmt="e4m3"):
    dtype, down = {"e4m3": (ml_dtypes.float8_e4m3fn, 7), "e5m2": (ml_dtypes.float8_e5m2, 14)}[fmt]
    v = np.moveaxis(np.asarray(x, np.float32).astype(ml_dtypes.bfloat16).astype(np.float64), axis, -1)
    blocks = v.reshape(v.shape[:-1] + (-1, 32))
    amax = np.abs(blocks).max(-1, keepdims=True)
    byte = np.maximum(np.where(amax > 0, np.frexp(amax)[1] - 1 + 127, 0) - down, 1)
    scale = np.exp2(byte - 127.0)
    codes = (blocks / scale).astype(np.float32).astype(dtype).astype(np.float64)
    return np.moveaxis((codes * scale).reshape(v.shape), -1, axis)


WIDE = False


def mx_kscale(k):
    if not WIDE:
        return np.ones(k)
    levels = np.array([10, -10, 5, -5, 0])
    if k % 512:
        return np.exp2(np.random.permutation(np.resize(levels, k // 32))).repeat(32)
    a = np.empty((k // 512, 16))
    for p in range(k // 512):
        a[p, :8] = np.random.permutation(np.resize(levels, 8))
        for g in range(8):
            far = levels[np.abs(levels - a[p, g]) >= 10]
            a[p, g + 8] = far[np.random.randint(len(far))]
    return np.exp2(a.ravel()).repeat(32)


def f64(x):
    return np.asarray(x).astype(np.float64)


def striped(idx):
    return np.tile(idx.reshape(-1, 16).T, (8, 1)).astype(np.uint16)


def unstriped(offs):
    return offs[:16].T.reshape(-1).astype(np.int64)


E2M1 = np.array([0.0, 0.5, 1.0, 1.5, 2.0, 3.0, 4.0, 6.0, -0.0, -0.5, -1.0, -1.5, -2.0, -3.0, -4.0, -6.0])


def pack_weight(w, fmt):
    k, n = w.shape
    w = f64(np.asarray(w, np.float32).astype(ml_dtypes.bfloat16)).reshape(k // 32, 32, n)
    amax = np.abs(w).max(1)
    if fmt == "e4m3":
        byte = np.frexp(amax)[1] - 1 + 127 - 7
    else:
        mant, ex = np.frexp(amax / 6.0)
        byte = np.where(mant > 0.5, ex, ex - 1) + 127
    byte = np.clip(np.where(amax > 0, byte, 1), 1, 254)
    scaled = (w * np.exp2(127.0 - byte)[:, None, :]).reshape(k, n).astype(np.float32)
    by_word = np.ascontiguousarray(scaled.reshape(k // 512, 128, 4, n).transpose(0, 1, 3, 2))
    if fmt == "e4m3":
        words = by_word.astype(ml_dtypes.float8_e4m3fn).view(np.uint8)
    else:
        c = by_word.astype(ml_dtypes.float4_e2m1fn).view(np.uint8) & 0xF
        words = (c[..., 0::2] | (c[..., 1::2] << 4)).reshape(k // 512, 128, 2 * n)
    return np.ascontiguousarray(words), np.ascontiguousarray(byte.astype(np.uint8).reshape(k // 512, 16, n))


def unpack_weight(words, scales, fmt):
    g, _, n = scales.shape
    words = np.ascontiguousarray(words).reshape(g, 128, n, -1)
    if fmt == "e4m3":
        vals = words.view(ml_dtypes.float8_e4m3fn).astype(np.float64)
    else:
        nib = np.empty((g, 128, n, 4), np.uint8)
        nib[..., 0::2] = words & 0xF
        nib[..., 1::2] = words >> 4
        vals = E2M1[nib]
    vals = vals * np.repeat(np.exp2(scales.astype(np.float64) - 127.0), 8, axis=1)[..., None]
    return vals.transpose(0, 1, 3, 2).reshape(g * 512, n)


def gelu(v):
    return 0.5 * v * (1.0 + np.tanh(np.sqrt(2.0 / np.pi) * (v + 0.044715 * v**3)))


def striped8(idx):
    return np.concatenate([v.reshape(-1, 16).T for v in idx]).astype(np.uint16)


def unstriped8(offs):
    return np.stack([offs[16 * g:16 * g + 16].T.reshape(-1) for g in range(8)]).astype(np.int64)


def heads(h, wgt, idx8):
    r = np.arange(h.shape[0])
    return wgt[r // 4 % 128] * h[r[:, None], idx8[r % 512 // 64]]


def put_heads(h, wgs, idx8, t2):
    r = np.arange(h.shape[0])
    page = np.zeros((h.shape[0], t2))
    page[r[:, None], idx8[r % 512 // 64]] = wgs[r // 4 % 128] * h
    return page


K, T, S, P, T2, H, N = 1024, 4096, 1024, 1024, 2048, 1024, 384

def setup_inputs():
    n = np.random.standard_normal
    s = mx_kscale(K)[:, None]
    u = mx_kscale(H)[:, None]
    d = {}
    d["tab_words"], d["tab_scales"] = pack_weight(n((K, T)) * s, "e4m3")
    d["offs"] = striped(np.random.permutation(T)[:S])
    d["offs2"] = striped8(np.stack([np.random.permutation(T2)[:S] for _ in range(8)]))
    d["offs3"] = striped8(np.stack([np.random.permutation(T2)[:P] for _ in range(8)]))
    d["w1"] = (2.0 * n((K, H)) / s / K ** 0.5).astype(np.float32)
    d["w2_words"], d["w2_scales"] = pack_weight(n((K, H)) / s / K ** 0.5, "e4m3")
    d["gain"] = (np.exp(0.4 * n(H)) * u[:, 0] ** 2).astype(np.float32)
    d["wgs"] = np.repeat(np.random.uniform(0.5, 2.0, (8, S)), 16, axis=0).astype(np.float32)
    d["wgt"] = np.repeat(np.random.uniform(0.5, 2.0, (8, P)), 16, axis=0).astype(np.float32)
    d["pace"] = (0.9 * n((H, P)) * u).astype(np.float32)
    d["w3_words"], d["w3_scales"] = pack_weight(n((H, N)) / u / H ** 0.5, "e2m1")
    return d

def reference(tab_words, tab_scales, offs, offs2, offs3, w1, w2_words, w2_scales, gain, wgs, wgt, pace, w3_words, w3_scales):
    v = unpack_weight(tab_words, tab_scales, "e4m3")[:, unstriped(offs)]
    bounded = np.tanh(mxq(f64(w1), 0, "e4m3").T @ v)
    plain = unpack_weight(w2_words, w2_scales, "e4m3").T @ v
    h = f64(gain)[:, None] * np.square(bounded - plain)
    page = put_heads(h, f64(wgs), unstriped8(offs2), T2)
    x = heads(page, f64(wgt), unstriped8(offs3))
    z = np.sqrt(x + np.square(f64(pace)))
    return unpack_weight(w3_words, w3_scales, "e2m1").T @ mxq(z, 0, "e4m3")

@@ -1,0 +1,300 @@
+from contextlib import ExitStack
+
+import concourse.mybir as mybir
+from concourse.masks import make_identity
+
+K, T, S, M, T2, H, N = 1024, 4096, 1024, 1024, 2048, 1024, 384
+FLOPS = 2 * (2 * K * H * S + H * N * M)
+
+F32 = mybir.dt.float32
+BF16 = mybir.dt.bfloat16
+I32 = mybir.dt.int32
+U32 = mybir.dt.uint32
+U16 = mybir.dt.uint16
+U8 = mybir.dt.uint8
+FP8X4 = mybir.dt.float8_e4m3fn_x4
+FP4X4 = mybir.dt.float4_e2m1fn_x4
+ACT = mybir.ActivationFunctionType
+ALU = mybir.AluOpType
+
+P = 128
+PACK = 4
+PASS = P * PACK
+BANK = 512
+HALF = 512
+CHUNK = 256
+
+
+def tile_list_handler_matching_features_kernel(
+    tc, tab_words, tab_scales, offs, offs2, offs3, w1, w2_words, w2_scales, gain, wgs, wgt, pace, w3_words, w3_scales, out
+):
+    nc = tc.nc
+    with ExitStack() as ctx:
+        lists = ctx.enter_context(tc.tile_pool(name="lists", bufs=1))
+        keep = ctx.enter_context(tc.tile_pool(name="keep", bufs=1))
+        ring = ctx.enter_context(tc.tile_pool(name="ring", bufs=1))
+        psum = ctx.enter_context(tc.psum_pool(name="psum", bufs=1))
+
+        def held(shape, dtype, name):
+            return keep.tile(shape, dtype, name=name, align_bytes=64)
+
+        def big(shape, dtype, name):
+            return ring.tile(shape, dtype, name=name, tag="big", bufs=2, align_bytes=64)
+
+        def mid(shape, dtype, name):
+            return ring.tile(shape, dtype, name=name, tag="mid", bufs=5, align_bytes=64)
+
+        def small(shape, dtype, name):
+            return ring.tile(shape, dtype, name=name, tag="small", bufs=16, align_bytes=64)
+
+        def bank(shape, name, tag, bufs):
+            return psum.tile(shape, F32, name=name, tag=tag, bufs=bufs)
+
+        def words(dram):
+            return dram.rearrange("p c i -> p (c i)").bitcast(I32)
+
+        def successor(shape, dtype, name, tag):
+            return ring.tile(shape, dtype, name=name, tag=tag, bufs=1, align_bytes=64)
+
+        tab_plane = successor([P, T], U8, "tab_plane", "plane_then_codes")
+        w2_plane = held([P, H], U8, "w2_plane")
+        w3_plane = held([P, 2, N], U8, "w3_plane")
+        for plane in (tab_plane[:], w3_plane[:].rearrange("p a n -> p (a n)")):
+            nc.vector.memset(plane.bitcast(I32), 0)
+        nc.gpsimd.memset(w2_plane[:].bitcast(I32), 0)
+
+        def load_packed_plane(queue, plane, scales):
+            for q in range(4):
+                queue.dma_start(
+                    out=plane[32 * q : 32 * q + 8, :].bitcast(I32), in_=scales[:, 4 * q : 4 * q + 4, :].bitcast(I32)
+                )
+
+        load_packed_plane(nc.gpsimd, w2_plane, w2_scales)
+        ident = held([P, P], F32, "ident")
+        make_identity(nc, ident[:])
+
+        idx = lists.tile([P, S // 16], U16, name="idx")
+        idx2 = lists.tile([P, S // 16], U16, name="idx2")
+        idx3 = lists.tile([P, M // 16], U16, name="idx3")
+        gain_sb = held([P, 2, PACK], F32, "gain_sb")
+        nc.sync.dma_start(idx[:], offs)
+        nc.sync.dma_start(out=gain_sb[:], in_=gain.rearrange("(b p i) -> p b i", b=2, i=PACK))
+        nc.sync.dma_start(idx2[:], offs2)
+        nc.sync.dma_start(idx3[:], offs3)
+
+        w1_raw = {}
+
+        def load_w1(a, b):
+            raw = ring.tile([P, PACK, PASS], F32, name=f"w1_raw{a}{b}", tag="w1_raw", bufs=2, align_bytes=64)
+            rows = w1[a * PASS : (a + 1) * PASS, b * PASS : (b + 1) * PASS]
+            nc.sync.dma_start(out=raw[:], in_=rows.rearrange("(p j) c -> p j c", j=PACK))
+            w1_raw[a, b] = raw
+
+        tab = [big([P, T], U32, f"tab{a}") for a in range(2)]
+        w2_codes = {(a, b): held([P, PASS], U32, f"w2_codes{a}{b}") for a in range(2) for b in range(2)}
+
+        def load_w2(a, b):
+            nc.sync.dma_start(out=w2_codes[a, b][:].bitcast(I32), in_=words(w2_words[a, :, b * PASS : (b + 1) * PASS, :]))
+
+        load_w1(0, 0)
+        load_packed_plane(nc.scalar, tab_plane, tab_scales)
+        for c in range(2):
+            cols = slice(c * T // 2, (c + 1) * T // 2)
+            nc.sync.dma_start(out=tab[0][:, cols].bitcast(I32), in_=words(tab_words[0, :, cols, :]))
+        load_w1(1, 0)
+        load_w2(0, 0)
+        nc.sync.dma_start(out=tab[1][:].bitcast(I32), in_=words(tab_words[1]))
+        load_w2(1, 0)
+        wgs_sb = held([P, S], F32, "wgs_sb")
+        nc.sync.dma_start(out=wgs_sb[:], in_=wgs)
+        load_w2(0, 1)
+        load_w2(1, 1)
+        wgt_sb = held([P, M], F32, "wgt_sb")
+        nc.sync.dma_start(out=wgt_sb[:], in_=wgt)
+        load_w1(0, 1)
+        load_w1(1, 1)
+        w3_codes = held([P, 2, 2 * N], U8, "w3_codes")
+        nc.sync.dma_start(out=w3_codes[:].bitcast(I32), in_=w3_words.rearrange("a p c -> p a c").bitcast(I32))
+        for q in range(4):
+            nc.sync.dma_start(
+                out=w3_plane[32 * q : 32 * q + 4, :, :].bitcast(I32),
+                in_=w3_scales[:, 4 * q : 4 * q + 4, :].rearrange("a r n -> r a n").bitcast(I32),
+            )
+
+        pages = [held([P, T2], F32, f"page{i}") for i in range(PACK)]
+        for page in pages:
+            nc.vector.memset(page[:], 0.0)
+
+        root0 = held([P, 2 * PACK], F32, "root0")
+        inv = held([P, 2 * PACK], F32, "inv")
+        quot = held([P, 2 * PACK], F32, "quot")
+        root = held([P, 2 * PACK], F32, "root")
+        zero = held([P, 1], F32, "zero")
+        gain_flat = gain_sb[:].rearrange("p b i -> p (b i)")
+        nc.scalar.activation(root0[:], gain_flat, ACT.Sqrt)
+        nc.scalar.activation(zero[:], root0[:, 0:1], ACT.Tanh, scale=0.0)
+        nc.vector.reciprocal(inv[:], root0[:])
+        nc.vector.scalar_tensor_tensor(quot[:], gain_flat, 0.5, inv[:], ALU.mult, ALU.mult)
+        nc.vector.scalar_tensor_tensor(root[:], root0[:], 0.5, quot[:], ALU.mult, ALU.add)
+
+        v_plane = held([P, S], U8, "v_plane")
+        v_codes, w1_codes = {}, {}
+        w1_plane = {(a, b): held([P, PASS], U8, f"w1_plane{a}{b}") for a in range(2) for b in range(2)}
+
+        def quantise_w1(a, b):
+            grouped = successor([P, PASS, PACK], BF16, f"w1_grouped{a}{b}", f"grouped{a}{b}")
+            if (a, b) == (1, 0):
+                w1_codes[a, b] = successor([P, PASS], U32, f"w1_codes{a}{b}", "plane_then_codes")
+            else:
+                w1_codes[a, b] = held([P, PASS], U32, f"w1_codes{a}{b}")
+            for c in range(2):
+                nc.scalar.copy(
+                    grouped[:, c * 256 : (c + 1) * 256, :].rearrange("p (g e) j -> p g j e", e=4),
+                    w1_raw[a, b][:, :, c * 256 : (c + 1) * 256].rearrange("p j (g e) -> p g j e", e=4),
+                )
+            nc.vector.quantize_mx(
+                out=w1_codes[a, b][:].bitcast(FP8X4), scales=w1_plane[a, b][:], in_=grouped[:].rearrange("p c j -> p (c j)")
+            )
+
+        nc.vector.tensor_copy(v_plane[:], tab_plane[:].indirect(idx[:]))
+        quantise_w1(0, 0)
+        v_codes[0] = successor([P, S], U32, "v_codes0", "grouped00")
+        nc.vector.tensor_copy(v_codes[0][:], tab[0][:].indirect(idx[:]))
+        quantise_w1(1, 0)
+        v_codes[1] = successor([P, S], U32, "v_codes1", "grouped10")
+        for h in range(2):
+            nc.vector.tensor_copy(
+                v_codes[1][:, h * HALF : (h + 1) * HALF], tab[1][:].indirect(idx[:, h * HALF // 16 : (h + 1) * HALF // 16])
+            )
+
+        pace_sb = []
+        for b in range(2):
+            tile_b = big([P, PACK, M], F32, f"pace{b}")
+            nc.sync.dma_start(out=tile_b[:], in_=pace[b * PASS : (b + 1) * PASS, :].rearrange("(p i) m -> p i m", i=PACK))
+            pace_sb.append(tile_b)
+
+
+        def first_stage(b, start, count, negate_on_vector=False):
+            tiles = count // P
+            bounded, negated = [], []
+            for t in range(tiles):
+                tokens = slice(start + t * P, start + (t + 1) * P)
+                acc1 = bank([P, BANK], "acc1", "a", 3)
+                acc2 = bank([P, BANK], "acc2", "b", 3)
+                for a in range(2):
+                    nc.tensor.matmul_mx(
+                        out=acc1[:], lhsT=v_codes[a][:, tokens].bitcast(FP8X4), lhsT_scale=v_plane[4 * a : P, tokens],
+                        rhs=w1_codes[a, b][:].bitcast(FP8X4), rhs_scale=w1_plane[a, b][:], start=(a == 0), stop=(a == 1),
+                    )
+                for a in range(2):
+                    nc.tensor.matmul_mx(
+                        out=acc2[:], lhsT=v_codes[a][:, tokens].bitcast(FP8X4), lhsT_scale=v_plane[4 * a : P, tokens],
+                        rhs=w2_codes[a, b][:].bitcast(FP8X4), rhs_scale=w2_plane[4 * a : P, b * PASS : (b + 1) * PASS],
+                        start=(a == 0), stop=(a == 1),
+                    )
+                tanh_t = small([P, PACK, P], F32, "tanh_t")
+                neg_t = small([P, PACK, P], F32, "neg_t")
+                nc.scalar.activation(tanh_t[:], acc1[:].rearrange("j (p i) -> j i p", i=PACK), ACT.Tanh, bias=zero[:])
+                if negate_on_vector:
+                    nc.vector.tensor_scalar_mul(neg_t[:], acc2[:].rearrange("j (p i) -> j i p", i=PACK), -1.0)
+                else:
+                    nc.scalar.activation(neg_t[:], acc2[:].rearrange("j (p i) -> j i p", i=PACK), ACT.Copy, scale=-1.0)
+                bounded.append(tanh_t)
+                negated.append(neg_t)
+            for i in range(PACK):
+                diff = bank([P, tiles, P], "diff", "d", 2)
+                for t in range(tiles):
+                    nc.tensor.matmul(diff[:, t, :], bounded[t][:, i, :], ident[:], start=True, stop=False, is_transpose=True)
+                    nc.tensor.matmul(diff[:, t, :], negated[t][:, i, :], ident[:], start=False, stop=True, is_transpose=True)
+                h_sb = ring.tile([P, count], F32, name="h_sb", tag="h", bufs=12, align_bytes=64)
+                col = b * PACK + i
+                nc.scalar.activation(h_sb[:], diff[:].rearrange("p t j -> p (t j)"), ACT.Square, scale=root[:, col : col + 1])
+                entries = slice(start // 16, (start + count) // 16)
+                nc.vector.tensor_tensor(pages[i][:].indirect(idx2[:, entries]), h_sb[:], wgs_sb[:, start : start + count], ALU.mult)
+
+        x_sb = {}
+
+        def shared(c, shape, name):
+            return ring.tile(shape, F32, name=name, tag=f"shared{c}", bufs=1, align_bytes=64)
+
+        def gather(b, c, start, count):
+            if b == 1:
+                x_c = shared(c, [P, PACK, count], f"x{b}{c}")
+            else:
+                x_c = mid([P, PACK, count], F32, f"x{b}{c}")
+            entries = slice(start // 16, (start + count) // 16)
+            for i in range(PACK):
+                nc.vector.tensor_tensor(x_c[:, i, :], pages[i][:].indirect(idx3[:, entries]), wgt_sb[:, start : start + count], ALU.mult)
+            x_sb[b, c] = x_c
+
+        z_codes = [held([P, M], U32, f"z_codes{b}") for b in range(2)]
+        z_plane = [held([P, M], U8, f"z_plane{b}") for b in range(2)]
+
+        def square_pace(b):
+            for i in range(PACK):
+                nc.scalar.activation(pace_sb[b][:, i, :], pace_sb[b][:, i, :], ACT.Square)
+
+        def second_operand(b, c, start, count):
+            tiles = count // P
+            z_t = small([P, tiles, 2, P, 2], BF16, "z_t")
+            for u in range(2):
+                total = bank([P, tiles, 2, P], "total", "a", 3)
+                for t in range(tiles):
+                    for e in range(2):
+                        i = 2 * u + e
+                        cols = slice(start + t * P, start + (t + 1) * P)
+                        nc.tensor.matmul(total[:, t, e, :], pace_sb[b][:, i, cols], ident[:], start=True, stop=False, is_transpose=True)
+                        nc.tensor.matmul(
+                            total[:, t, e, :], x_sb[b, c][:, i, t * P : (t + 1) * P], ident[:], start=False, stop=True, is_transpose=True
+                        )
+                nc.scalar.activation(z_t[:, :, u, :, :], total[:].rearrange("m t e p -> m t p e"), ACT.Sqrt)
+            z_words = z_t[:].rearrange("m t u p e -> m (t u p e)").bitcast(F32)
+            back = bank([P, 2, count], "back", "b", 3)
+            for t in range(tiles):
+                for u in range(2):
+                    nc.tensor.transpose(back[:, u, t * P : (t + 1) * P], z_words[:, (2 * t + u) * P : (2 * t + u + 1) * P], ident[:])
+            if b == 0:
+                z_grouped = shared(c, [P, count, 2], "z_grouped0")
+            else:
+                z_grouped = small([P, count, 2], F32, "z_grouped1")
+            nc.scalar.copy(z_grouped[:], back[:].rearrange("p u m -> p m u"))
+            cols = slice(start, start + count)
+            nc.vector.quantize_mx(
+                out=z_codes[b][:, cols].bitcast(FP8X4), scales=z_plane[b][:, cols],
+                in_=z_grouped[:].rearrange("p m u -> p (m u)").bitcast(BF16),
+            )
+
+        def last_product(start, count):
+            for t in range(count // P):
+                cols = slice(start + t * P, start + (t + 1) * P)
+                res = bank([P, N // P, P], "res", "d", 2)
+                for nt in range(N // P):
+                    for b in range(2):
+                        nc.tensor.matmul_mx(
+                            out=res[:, nt, :], lhsT=w3_codes[:, b, 2 * nt * P : 2 * (nt + 1) * P].bitcast(FP4X4),
+                            lhsT_scale=w3_plane[:, b, nt * P : (nt + 1) * P],
+                            rhs=z_codes[b][:, cols].bitcast(FP8X4), rhs_scale=z_plane[b][:, cols], start=(b == 0), stop=(b == 1),
+                        )
+                res_sb = small([P, N // P, P], F32, "res_sb")
+                nc.vector.tensor_copy(res_sb[:], res[:])
+                nc.sync.dma_start(out=out[:, cols].rearrange("(nt p) m -> p nt m", p=P), in_=res_sb[:])
+
+        tapered = [(0, 256), (256, 256), (512, 256), (768, 128), (896, 128)]
+        first_stage(0, 0, 256, negate_on_vector=True)
+        first_stage(0, 256, 256)
+        first_stage(0, 512, 512)
+        quantise_w1(0, 1)
+        quantise_w1(1, 1)
+        for c, (start, count) in enumerate(tapered):
+            gather(0, c, start, count)
+        first_stage(1, 0, 512)
+        first_stage(1, 512, 512)
+        square_pace(0)
+        for c, (start, count) in enumerate(tapered):
+            second_operand(0, c, start, count)
+        square_pace(1)
+        for c, (start, count) in enumerate(tapered):
+            gather(1, c, start, count)
+        for c, (start, count) in enumerate(tapered):
+            second_operand(1, c, start, count)
+            last_product(start, count)

@@ -38,12 +38,6 @@ def tile_list_handler_matching_features_kernel(
         def held(shape, dtype, name):
             return keep.tile(shape, dtype, name=name, align_bytes=64)
 
-        def big(shape, dtype, name):
-            return ring.tile(shape, dtype, name=name, tag="big", bufs=2, align_bytes=64)
-
-        def mid(shape, dtype, name):
-            return ring.tile(shape, dtype, name=name, tag="mid", bufs=5, align_bytes=64)
-
         def small(shape, dtype, name):
             return ring.tile(shape, dtype, name=name, tag="small", bufs=16, align_bytes=64)
 
@@ -59,9 +53,8 @@ def tile_list_handler_matching_features_kernel(
         tab_plane = successor([P, T], U8, "tab_plane", "plane_then_codes")
         w2_plane = held([P, H], U8, "w2_plane")
         w3_plane = held([P, 2, N], U8, "w3_plane")
-        for plane in (tab_plane[:], w3_plane[:].rearrange("p a n -> p (a n)")):
+        for plane in (tab_plane[:], w2_plane[:], w3_plane[:].rearrange("p a n -> p (a n)")):
             nc.vector.memset(plane.bitcast(I32), 0)
-        nc.gpsimd.memset(w2_plane[:].bitcast(I32), 0)
 
         def load_packed_plane(queue, plane, scales):
             for q in range(4):
@@ -69,7 +62,6 @@ def tile_list_handler_matching_features_kernel(
                     out=plane[32 * q : 32 * q + 8, :].bitcast(I32), in_=scales[:, 4 * q : 4 * q + 4, :].bitcast(I32)
                 )
 
-        load_packed_plane(nc.gpsimd, w2_plane, w2_scales)
         ident = held([P, P], F32, "ident")
         make_identity(nc, ident[:])
 
@@ -84,25 +76,28 @@ def tile_list_handler_matching_features_kernel(
 
         w1_raw = {}
 
-        def load_w1(a, b):
+        def load_w1(a, b, pieces=1):
             raw = ring.tile([P, PACK, PASS], F32, name=f"w1_raw{a}{b}", tag="w1_raw", bufs=2, align_bytes=64)
             rows = w1[a * PASS : (a + 1) * PASS, b * PASS : (b + 1) * PASS]
-            nc.sync.dma_start(out=raw[:], in_=rows.rearrange("(p j) c -> p j c", j=PACK))
+            for j in range(0, PACK, PACK // pieces):
+                part = slice(j, j + PACK // pieces)
+                nc.sync.dma_start(out=raw[:, part, :], in_=rows.rearrange("(p j) c -> p j c", j=PACK)[:, part, :])
             w1_raw[a, b] = raw
 
-        tab = [big([P, T], U32, f"tab{a}") for a in range(2)]
+        tab = [successor([P, T], U32, f"tab{a}", f"table_then_pace{a}") for a in range(2)]
         w2_codes = {(a, b): held([P, PASS], U32, f"w2_codes{a}{b}") for a in range(2) for b in range(2)}
 
         def load_w2(a, b):
             nc.sync.dma_start(out=w2_codes[a, b][:].bitcast(I32), in_=words(w2_words[a, :, b * PASS : (b + 1) * PASS, :]))
 
-        load_w1(0, 0)
-        load_packed_plane(nc.scalar, tab_plane, tab_scales)
-        for c in range(2):
-            cols = slice(c * T // 2, (c + 1) * T // 2)
+        load_w1(0, 0, pieces=4)
+        load_packed_plane(nc.sync, tab_plane, tab_scales)
+        load_w2(0, 0)
+        for c in range(4):
+            cols = slice(c * T // 4, (c + 1) * T // 4)
             nc.sync.dma_start(out=tab[0][:, cols].bitcast(I32), in_=words(tab_words[0, :, cols, :]))
         load_w1(1, 0)
-        load_w2(0, 0)
+        load_packed_plane(nc.sync, w2_plane, w2_scales)
         nc.sync.dma_start(out=tab[1][:].bitcast(I32), in_=words(tab_words[1]))
         load_w2(1, 0)
         wgs_sb = held([P, S], F32, "wgs_sb")
@@ -123,7 +118,7 @@ def tile_list_handler_matching_features_kernel(
 
         pages = [held([P, T2], F32, f"page{i}") for i in range(PACK)]
         for page in pages:
-            nc.vector.memset(page[:], 0.0)
+            nc.gpsimd.memset(page[:], 0.0)
 
         root0 = held([P, 2 * PACK], F32, "root0")
         inv = held([P, 2 * PACK], F32, "inv")
@@ -138,14 +133,15 @@ def tile_list_handler_matching_features_kernel(
         nc.vector.scalar_tensor_tensor(root[:], root0[:], 0.5, quot[:], ALU.mult, ALU.add)
 
         v_plane = held([P, S], U8, "v_plane")
-        v_codes, w1_codes = {}, {}
-        w1_plane = {(a, b): held([P, PASS], U8, f"w1_plane{a}{b}") for a in range(2) for b in range(2)}
+        v_codes, w1_codes, w1_plane = {}, {}, {}
 
         def quantise_w1(a, b):
             grouped = successor([P, PASS, PACK], BF16, f"w1_grouped{a}{b}", f"grouped{a}{b}")
             if (a, b) == (1, 0):
                 w1_codes[a, b] = successor([P, PASS], U32, f"w1_codes{a}{b}", "plane_then_codes")
+                w1_plane[a, b] = successor([P, PASS], U8, f"w1_plane{a}{b}", "table_then_pace0")
             else:
+                w1_plane[a, b] = held([P, PASS], U8, f"w1_plane{a}{b}")
                 w1_codes[a, b] = held([P, PASS], U32, f"w1_codes{a}{b}")
             for c in range(2):
                 nc.scalar.copy(
@@ -167,20 +163,13 @@ def tile_list_handler_matching_features_kernel(
                 v_codes[1][:, h * HALF : (h + 1) * HALF], tab[1][:].indirect(idx[:, h * HALF // 16 : (h + 1) * HALF // 16])
             )
 
-        pace_sb = []
-        for b in range(2):
-            tile_b = big([P, PACK, M], F32, f"pace{b}")
-            nc.sync.dma_start(out=tile_b[:], in_=pace[b * PASS : (b + 1) * PASS, :].rearrange("(p i) m -> p i m", i=PACK))
-            pace_sb.append(tile_b)
-
-
-        def first_stage(b, start, count, negate_on_vector=False):
+        def first_stage(b, start, count, negate_on_vector=False, after_first_pair=None):
             tiles = count // P
             bounded, negated = [], []
             for t in range(tiles):
                 tokens = slice(start + t * P, start + (t + 1) * P)
-                acc1 = bank([P, BANK], "acc1", "a", 3)
-                acc2 = bank([P, BANK], "acc2", "b", 3)
+                acc1 = bank([P, BANK], "acc1", "a", 2)
+                acc2 = bank([P, BANK], "acc2", "b", 2)
                 for a in range(2):
                     nc.tensor.matmul_mx(
                         out=acc1[:], lhsT=v_codes[a][:, tokens].bitcast(FP8X4), lhsT_scale=v_plane[4 * a : P, tokens],
@@ -202,7 +191,7 @@ def tile_list_handler_matching_features_kernel(
                 bounded.append(tanh_t)
                 negated.append(neg_t)
             for i in range(PACK):
-                diff = bank([P, tiles, P], "diff", "d", 2)
+                diff = bank([P, tiles, P], "diff", "d", 4)
                 for t in range(tiles):
                     nc.tensor.matmul(diff[:, t, :], bounded[t][:, i, :], ident[:], start=True, stop=False, is_transpose=True)
                     nc.tensor.matmul(diff[:, t, :], negated[t][:, i, :], ident[:], start=False, stop=True, is_transpose=True)
@@ -211,21 +200,13 @@ def tile_list_handler_matching_features_kernel(
                 nc.scalar.activation(h_sb[:], diff[:].rearrange("p t j -> p (t j)"), ACT.Square, scale=root[:, col : col + 1])
                 entries = slice(start // 16, (start + count) // 16)
                 nc.vector.tensor_tensor(pages[i][:].indirect(idx2[:, entries]), h_sb[:], wgs_sb[:, start : start + count], ALU.mult)
+                if i == 1 and after_first_pair is not None:
+                    after_first_pair()
 
-        x_sb = {}
 
-        def shared(c, shape, name):
-            return ring.tile(shape, F32, name=name, tag=f"shared{c}", bufs=1, align_bytes=64)
-
-        def gather(b, c, start, count):
-            if b == 1:
-                x_c = shared(c, [P, PACK, count], f"x{b}{c}")
-            else:
-                x_c = mid([P, PACK, count], F32, f"x{b}{c}")
+        def gather(x_row, i, start, count):
             entries = slice(start // 16, (start + count) // 16)
-            for i in range(PACK):
-                nc.vector.tensor_tensor(x_c[:, i, :], pages[i][:].indirect(idx3[:, entries]), wgt_sb[:, start : start + count], ALU.mult)
-            x_sb[b, c] = x_c
+            nc.vector.tensor_tensor(x_row, pages[i][:].indirect(idx3[:, entries]), wgt_sb[:, start : start + count], ALU.mult)
 
         z_codes = [held([P, M], U32, f"z_codes{b}") for b in range(2)]
         z_plane = [held([P, M], U8, f"z_plane{b}") for b in range(2)]
@@ -234,67 +215,112 @@ def tile_list_handler_matching_features_kernel(
             for i in range(PACK):
                 nc.scalar.activation(pace_sb[b][:, i, :], pace_sb[b][:, i, :], ACT.Square)
 
-        def second_operand(b, c, start, count):
+        def roots_by_transposes(b, pairs, x_tile, start, count, staged):
             tiles = count // P
-            z_t = small([P, tiles, 2, P, 2], BF16, "z_t")
-            for u in range(2):
-                total = bank([P, tiles, 2, P], "total", "a", 3)
-                for t in range(tiles):
-                    for e in range(2):
-                        i = 2 * u + e
-                        cols = slice(start + t * P, start + (t + 1) * P)
-                        nc.tensor.matmul(total[:, t, e, :], pace_sb[b][:, i, cols], ident[:], start=True, stop=False, is_transpose=True)
-                        nc.tensor.matmul(
-                            total[:, t, e, :], x_sb[b, c][:, i, t * P : (t + 1) * P], ident[:], start=False, stop=True, is_transpose=True
-                        )
+            z_t = small([P, tiles, pairs, P, 2], BF16, "z_t")
+            for u in range(pairs):
+                total = bank([P, tiles, 2, P], "total", "d", 4)
+                for n, source in enumerate((pace_sb[b], x_tile)):
+                    for t in range(tiles):
+                        for e in range(2):
+                            nc.tensor.matmul(
+                                total[:, t, e, :], source[:, 2 * u + e, start + t * P : start + (t + 1) * P], ident[:],
+                                start=((n, t, e) == (0, 0, 0)), stop=((n, t, e) == (1, tiles - 1, 1)), is_transpose=True,
+                            )
                 nc.scalar.activation(z_t[:, :, u, :, :], total[:].rearrange("m t e p -> m t p e"), ACT.Sqrt)
             z_words = z_t[:].rearrange("m t u p e -> m (t u p e)").bitcast(F32)
-            back = bank([P, 2, count], "back", "b", 3)
+            back = bank([P, pairs, count], "back", "b", 2)
             for t in range(tiles):
-                for u in range(2):
-                    nc.tensor.transpose(back[:, u, t * P : (t + 1) * P], z_words[:, (2 * t + u) * P : (2 * t + u + 1) * P], ident[:])
-            if b == 0:
-                z_grouped = shared(c, [P, count, 2], "z_grouped0")
-            else:
-                z_grouped = small([P, count, 2], F32, "z_grouped1")
-            nc.scalar.copy(z_grouped[:], back[:].rearrange("p u m -> p m u"))
+                for u in range(pairs):
+                    block = pairs * t + u
+                    nc.tensor.transpose(back[:, u, t * P : (t + 1) * P], z_words[:, block * P : (block + 1) * P], ident[:])
+            staged_words = staged.rearrange("p m i -> p (m i)").bitcast(F32).rearrange("p (m u) -> p m u", u=2)
+            nc.scalar.copy(staged_words[:, :, 0:pairs], back[:].rearrange("p u m -> p m u"))
+
+        def quantise_z(b, start, count, staged):
             cols = slice(start, start + count)
             nc.vector.quantize_mx(
-                out=z_codes[b][:, cols].bitcast(FP8X4), scales=z_plane[b][:, cols],
-                in_=z_grouped[:].rearrange("p m u -> p (m u)").bitcast(BF16),
+                out=z_codes[b][:, cols].bitcast(FP8X4), scales=z_plane[b][:, cols], in_=staged.rearrange("p m i -> p (m i)")
             )
 
+        result_banks = [("d", 4)] * 4 + [("a", 2)] * 2 + [("b", 2)] * 2
+
         def last_product(start, count):
-            for t in range(count // P):
-                cols = slice(start + t * P, start + (t + 1) * P)
-                res = bank([P, N // P, P], "res", "d", 2)
-                for nt in range(N // P):
-                    for b in range(2):
+            for first in range(start, start + count, P):
+                cols = slice(first, first + P)
+                res = bank([P, N // P, P], "res", *result_banks[first // P])
+                for b in range(2):
+                    for nt in range(N // P):
                         nc.tensor.matmul_mx(
                             out=res[:, nt, :], lhsT=w3_codes[:, b, 2 * nt * P : 2 * (nt + 1) * P].bitcast(FP4X4),
                             lhsT_scale=w3_plane[:, b, nt * P : (nt + 1) * P],
-                            rhs=z_codes[b][:, cols].bitcast(FP8X4), rhs_scale=z_plane[b][:, cols], start=(b == 0), stop=(b == 1),
+                            rhs=z_codes[b][:, cols].bitcast(FP8X4), rhs_scale=z_plane[b][:, cols],
+                            start=(b == 0 and nt == 0), stop=(b == 1 and nt == N // P - 1),
                         )
                 res_sb = small([P, N // P, P], F32, "res_sb")
-                nc.vector.tensor_copy(res_sb[:], res[:])
+                if first >= 768:
+                    nc.vector.tensor_copy(res_sb[:], res[:])
+                else:
+                    nc.scalar.copy(res_sb[:], res[:])
                 nc.sync.dma_start(out=out[:, cols].rearrange("(nt p) m -> p nt m", p=P), in_=res_sb[:])
 
-        tapered = [(0, 256), (256, 256), (512, 256), (768, 128), (896, 128)]
-        first_stage(0, 0, 256, negate_on_vector=True)
+        first_stage(0, 0, 128, negate_on_vector=True)
+        first_stage(0, 128, 128, negate_on_vector=True)
         first_stage(0, 256, 256)
         first_stage(0, 512, 512)
+        pace_sb = []
+        for b in range(2):
+            tile_b = successor([P, PACK, M], F32, f"pace{b}", f"table_then_pace{b}")
+            nc.sync.dma_start(out=tile_b[:], in_=pace[b * PASS : (b + 1) * PASS, :].rearrange("(p i) m -> p i m", i=PACK))
+            pace_sb.append(tile_b)
         quantise_w1(0, 1)
         quantise_w1(1, 1)
-        for c, (start, count) in enumerate(tapered):
-            gather(0, c, start, count)
+        x0 = held([P, PACK, M], F32, "x0")
+        for start in range(0, M, HALF):
+            for i in range(PACK):
+                gather(x0[:, i, start : start + HALF], i, start, HALF)
+        x1 = held([P, 2, M], F32, "x1")
+
+        def gather_first_pair():
+            for start in range(0, M, HALF):
+                for i in range(2):
+                    gather(x1[:, i, start : start + HALF], i, start, HALF)
+
         first_stage(1, 0, 512)
-        first_stage(1, 512, 512)
+        first_stage(1, 512, 512, after_first_pair=gather_first_pair)
         square_pace(0)
-        for c, (start, count) in enumerate(tapered):
-            second_operand(0, c, start, count)
+        staged0 = successor([P, M, PACK], BF16, "staged0", "lag_a")
+        for start in range(0, M, CHUNK):
+            roots_by_transposes(0, 2, x0, start, CHUNK, staged0[:, start : start + CHUNK, :])
+            quantise_z(0, start, CHUNK, staged0[:, start : start + CHUNK, :])
         square_pace(1)
+        tapered = [(0, 256), (256, 256), (512, 256), (768, 128), (896, 128)]
+        staged1 = [successor([P, count, PACK], BF16, f"staged1{c}", f"lag_{c}") for c, (start, count) in enumerate(tapered)]
         for c, (start, count) in enumerate(tapered):
-            gather(1, c, start, count)
-        for c, (start, count) in enumerate(tapered):
-            second_operand(1, c, start, count)
+            roots_by_transposes(1, 1, x1, start, count, staged1[c][:])
+
+        def gather_and_add(x_rows, start, count):
+            for e in range(2):
+                gather(x_rows[:, e, :], 2 + e, start, count)
+            for e in range(2):
+                nc.vector.tensor_tensor(x_rows[:, e, :], x_rows[:, e, :], pace_sb[1][:, 2 + e, start : start + count], ALU.add)
+
+        def finish(c, x_rows):
+            start, count = tapered[c]
+            nc.scalar.activation(staged1[c][:, :, 2:4], x_rows.rearrange("p e m -> p m e"), ACT.Sqrt)
+            quantise_z(1, start, count, staged1[c][:])
             last_product(start, count)
+
+        x_a = successor([P, 2, 2, 256], F32, "x_a", "lag_a")
+        gather_and_add(x_a[:, 0], *tapered[0])
+        gather_and_add(x_a[:, 1], *tapered[1])
+        finish(0, x_a[:, 0])
+        x_b = successor([P, 2, 256], F32, "x_b", "lag_0")
+        gather_and_add(x_b[:], *tapered[2])
+        finish(1, x_a[:, 1])
+        x_c = successor([P, 2, 2, 128], F32, "x_c", "lag_1")
+        gather_and_add(x_c[:, 0], *tapered[3])
+        gather_and_add(x_c[:, 1], *tapered[4])
+        finish(2, x_b[:])
+        finish(3, x_c[:, 0])
+        finish(4, x_c[:, 1])

@@ -56,9 +56,9 @@ def tile_list_handler_matching_features_kernel(
         for plane in (tab_plane[:], w2_plane[:], w3_plane[:].rearrange("p a n -> p (a n)")):
             nc.vector.memset(plane.bitcast(I32), 0)
 
-        def load_packed_plane(queue, plane, scales):
+        def load_packed_plane(plane, scales):
             for q in range(4):
-                queue.dma_start(
+                nc.sync.dma_start(
                     out=plane[32 * q : 32 * q + 8, :].bitcast(I32), in_=scales[:, 4 * q : 4 * q + 4, :].bitcast(I32)
                 )
 
@@ -91,13 +91,13 @@ def tile_list_handler_matching_features_kernel(
             nc.sync.dma_start(out=w2_codes[a, b][:].bitcast(I32), in_=words(w2_words[a, :, b * PASS : (b + 1) * PASS, :]))
 
         load_w1(0, 0, pieces=4)
-        load_packed_plane(nc.sync, tab_plane, tab_scales)
+        load_packed_plane(tab_plane, tab_scales)
         load_w2(0, 0)
         for c in range(4):
             cols = slice(c * T // 4, (c + 1) * T // 4)
             nc.sync.dma_start(out=tab[0][:, cols].bitcast(I32), in_=words(tab_words[0, :, cols, :]))
         load_w1(1, 0)
-        load_packed_plane(nc.sync, w2_plane, w2_scales)
+        load_packed_plane(w2_plane, w2_scales)
         nc.sync.dma_start(out=tab[1][:].bitcast(I32), in_=words(tab_words[1]))
         load_w2(1, 0)
         wgs_sb = held([P, S], F32, "wgs_sb")
@@ -158,10 +158,8 @@ def tile_list_handler_matching_features_kernel(
         nc.vector.tensor_copy(v_codes[0][:], tab[0][:].indirect(idx[:]))
         quantise_w1(1, 0)
         v_codes[1] = successor([P, S], U32, "v_codes1", "grouped10")
-        for h in range(2):
-            nc.vector.tensor_copy(
-                v_codes[1][:, h * HALF : (h + 1) * HALF], tab[1][:].indirect(idx[:, h * HALF // 16 : (h + 1) * HALF // 16])
-            )
+        for start in range(0, S, HALF):
+            nc.vector.tensor_copy(v_codes[1][:, start : start + HALF], tab[1][:].indirect(idx[:, start // 16 : (start + HALF) // 16]))
 
         def first_stage(b, start, count, negate_on_vector=False, after_first_pair=None):
             tiles = count // P
@@ -203,7 +201,6 @@ def tile_list_handler_matching_features_kernel(
                 if i == 1 and after_first_pair is not None:
                     after_first_pair()
 
-
         def gather(x_row, i, start, count):
             entries = slice(start // 16, (start + count) // 16)
             nc.vector.tensor_tensor(x_row, pages[i][:].indirect(idx3[:, entries]), wgt_sb[:, start : start + count], ALU.mult)
@@ -232,8 +229,8 @@ def tile_list_handler_matching_features_kernel(
             back = bank([P, pairs, count], "back", "b", 2)
             for t in range(tiles):
                 for u in range(pairs):
-                    block = pairs * t + u
-                    nc.tensor.transpose(back[:, u, t * P : (t + 1) * P], z_words[:, block * P : (block + 1) * P], ident[:])
+                    place = pairs * t + u
+                    nc.tensor.transpose(back[:, u, t * P : (t + 1) * P], z_words[:, place * P : (place + 1) * P], ident[:])
             staged_words = staged.rearrange("p m i -> p (m i)").bitcast(F32).rearrange("p (m u) -> p m u", u=2)
             nc.scalar.copy(staged_words[:, :, 0:pairs], back[:].rearrange("p u m -> p m u"))
 
@@ -258,7 +255,7 @@ def tile_list_handler_matching_features_kernel(
                             start=(b == 0 and nt == 0), stop=(b == 1 and nt == N // P - 1),
                         )
                 res_sb = small([P, N // P, P], F32, "res_sb")
-                if first >= 768:
+                if first >= M - 2 * P:
                     nc.vector.tensor_copy(res_sb[:], res[:])
                 else:
                     nc.scalar.copy(res_sb[:], res[:])
@@ -318,9 +315,10 @@ def tile_list_handler_matching_features_kernel(
         x_b = successor([P, 2, 256], F32, "x_b", "lag_0")
         gather_and_add(x_b[:], *tapered[2])
         finish(1, x_a[:, 1])
-        x_c = successor([P, 2, 2, 128], F32, "x_c", "lag_1")
-        gather_and_add(x_c[:, 0], *tapered[3])
-        gather_and_add(x_c[:, 1], *tapered[4])
+        x_c = successor([P, 2, 128], F32, "x_c", "lag_1")
+        gather_and_add(x_c[:], *tapered[3])
         finish(2, x_b[:])
-        finish(3, x_c[:, 0])
-        finish(4, x_c[:, 1])
+        x_d = successor([P, 2, 128], F32, "x_d", "lag_2")
+        gather_and_add(x_d[:], *tapered[4])
+        finish(3, x_c[:])
+        finish(4, x_d[:])

from contextlib import ExitStack

import concourse.mybir as mybir
from concourse.masks import make_identity

K, T, S, M, T2, H, N = 1024, 4096, 1024, 1024, 2048, 1024, 384
FLOPS = 2 * (2 * K * H * S + H * N * M)

F32 = mybir.dt.float32
BF16 = mybir.dt.bfloat16
I32 = mybir.dt.int32
U32 = mybir.dt.uint32
U16 = mybir.dt.uint16
U8 = mybir.dt.uint8
FP8X4 = mybir.dt.float8_e4m3fn_x4
FP4X4 = mybir.dt.float4_e2m1fn_x4
ACT = mybir.ActivationFunctionType
ALU = mybir.AluOpType

P = 128
PACK = 4
PASS = P * PACK
BANK = 512
HALF = 512
CHUNK = 256


def tile_list_handler_matching_features_kernel(
    tc, tab_words, tab_scales, offs, offs2, offs3, w1, w2_words, w2_scales, gain, wgs, wgt, pace, w3_words, w3_scales, out
):
    nc = tc.nc
    with ExitStack() as ctx:
        lists = ctx.enter_context(tc.tile_pool(name="lists", bufs=1))
        keep = ctx.enter_context(tc.tile_pool(name="keep", bufs=1))
        ring = ctx.enter_context(tc.tile_pool(name="ring", bufs=1))
        psum = ctx.enter_context(tc.psum_pool(name="psum", bufs=1))

        def held(shape, dtype, name):
            return keep.tile(shape, dtype, name=name, align_bytes=64)

        def small(shape, dtype, name):
            return ring.tile(shape, dtype, name=name, tag="small", bufs=16, align_bytes=64)

        def bank(shape, name, tag, bufs):
            return psum.tile(shape, F32, name=name, tag=tag, bufs=bufs)

        def words(dram):
            return dram.rearrange("p c i -> p (c i)").bitcast(I32)

        def successor(shape, dtype, name, tag):
            return ring.tile(shape, dtype, name=name, tag=tag, bufs=1, align_bytes=64)

        tab_plane = successor([P, T], U8, "tab_plane", "plane_then_codes")
        w2_plane = held([P, H], U8, "w2_plane")
        w3_plane = held([P, 2, N], U8, "w3_plane")
        for plane in (tab_plane[:], w2_plane[:], w3_plane[:].rearrange("p a n -> p (a n)")):
            nc.vector.memset(plane.bitcast(I32), 0)

        def load_packed_plane(plane, scales):
            for q in range(4):
                nc.sync.dma_start(
                    out=plane[32 * q : 32 * q + 8, :].bitcast(I32), in_=scales[:, 4 * q : 4 * q + 4, :].bitcast(I32)
                )

        ident = held([P, P], F32, "ident")
        make_identity(nc, ident[:])

        idx = lists.tile([P, S // 16], U16, name="idx")
        idx2 = lists.tile([P, S // 16], U16, name="idx2")
        idx3 = lists.tile([P, M // 16], U16, name="idx3")
        gain_sb = held([P, 2, PACK], F32, "gain_sb")
        nc.sync.dma_start(idx[:], offs)
        nc.sync.dma_start(out=gain_sb[:], in_=gain.rearrange("(b p i) -> p b i", b=2, i=PACK))
        nc.sync.dma_start(idx2[:], offs2)
        nc.sync.dma_start(idx3[:], offs3)

        w1_raw = {}

        def load_w1(a, b, pieces=1):
            raw = ring.tile([P, PACK, PASS], F32, name=f"w1_raw{a}{b}", tag="w1_raw", bufs=2, align_bytes=64)
            rows = w1[a * PASS : (a + 1) * PASS, b * PASS : (b + 1) * PASS]
            for j in range(0, PACK, PACK // pieces):
                part = slice(j, j + PACK // pieces)
                nc.sync.dma_start(out=raw[:, part, :], in_=rows.rearrange("(p j) c -> p j c", j=PACK)[:, part, :])
            w1_raw[a, b] = raw

        tab = [successor([P, T], U32, f"tab{a}", f"table_then_pace{a}") for a in range(2)]
        w2_codes = {(a, b): held([P, PASS], U32, f"w2_codes{a}{b}") for a in range(2) for b in range(2)}

        def load_w2(a, b):
            nc.sync.dma_start(out=w2_codes[a, b][:].bitcast(I32), in_=words(w2_words[a, :, b * PASS : (b + 1) * PASS, :]))

        load_w1(0, 0, pieces=4)
        load_packed_plane(tab_plane, tab_scales)
        load_w2(0, 0)
        for c in range(4):
            cols = slice(c * T // 4, (c + 1) * T // 4)
            nc.sync.dma_start(out=tab[0][:, cols].bitcast(I32), in_=words(tab_words[0, :, cols, :]))
        load_w1(1, 0)
        load_packed_plane(w2_plane, w2_scales)
        nc.sync.dma_start(out=tab[1][:].bitcast(I32), in_=words(tab_words[1]))
        load_w2(1, 0)
        wgs_sb = held([P, S], F32, "wgs_sb")
        nc.sync.dma_start(out=wgs_sb[:], in_=wgs)
        load_w2(0, 1)
        load_w2(1, 1)
        wgt_sb = held([P, M], F32, "wgt_sb")
        nc.sync.dma_start(out=wgt_sb[:], in_=wgt)
        load_w1(0, 1)
        load_w1(1, 1)
        w3_codes = held([P, 2, 2 * N], U8, "w3_codes")
        nc.sync.dma_start(out=w3_codes[:].bitcast(I32), in_=w3_words.rearrange("a p c -> p a c").bitcast(I32))
        for q in range(4):
            nc.sync.dma_start(
                out=w3_plane[32 * q : 32 * q + 4, :, :].bitcast(I32),
                in_=w3_scales[:, 4 * q : 4 * q + 4, :].rearrange("a r n -> r a n").bitcast(I32),
            )

        pages = [held([P, T2], F32, f"page{i}") for i in range(PACK)]
        for page in pages:
            nc.gpsimd.memset(page[:], 0.0)

        root0 = held([P, 2 * PACK], F32, "root0")
        inv = held([P, 2 * PACK], F32, "inv")
        quot = held([P, 2 * PACK], F32, "quot")
        root = held([P, 2 * PACK], F32, "root")
        zero = held([P, 1], F32, "zero")
        gain_flat = gain_sb[:].rearrange("p b i -> p (b i)")
        nc.scalar.activation(root0[:], gain_flat, ACT.Sqrt)
        nc.scalar.activation(zero[:], root0[:, 0:1], ACT.Tanh, scale=0.0)
        nc.vector.reciprocal(inv[:], root0[:])
        nc.vector.scalar_tensor_tensor(quot[:], gain_flat, 0.5, inv[:], ALU.mult, ALU.mult)
        nc.vector.scalar_tensor_tensor(root[:], root0[:], 0.5, quot[:], ALU.mult, ALU.add)

        v_plane = held([P, S], U8, "v_plane")
        v_codes, w1_codes, w1_plane = {}, {}, {}

        def quantise_w1(a, b):
            grouped = successor([P, PASS, PACK], BF16, f"w1_grouped{a}{b}", f"grouped{a}{b}")
            if (a, b) == (1, 0):
                w1_codes[a, b] = successor([P, PASS], U32, f"w1_codes{a}{b}", "plane_then_codes")
                w1_plane[a, b] = successor([P, PASS], U8, f"w1_plane{a}{b}", "table_then_pace0")
            else:
                w1_plane[a, b] = held([P, PASS], U8, f"w1_plane{a}{b}")
                w1_codes[a, b] = held([P, PASS], U32, f"w1_codes{a}{b}")
            for c in range(2):
                nc.scalar.copy(
                    grouped[:, c * 256 : (c + 1) * 256, :].rearrange("p (g e) j -> p g j e", e=4),
                    w1_raw[a, b][:, :, c * 256 : (c + 1) * 256].rearrange("p j (g e) -> p g j e", e=4),
                )
            nc.vector.quantize_mx(
                out=w1_codes[a, b][:].bitcast(FP8X4), scales=w1_plane[a, b][:], in_=grouped[:].rearrange("p c j -> p (c j)")
            )

        nc.vector.tensor_copy(v_plane[:], tab_plane[:].indirect(idx[:]))
        quantise_w1(0, 0)
        v_codes[0] = successor([P, S], U32, "v_codes0", "grouped00")
        nc.vector.tensor_copy(v_codes[0][:], tab[0][:].indirect(idx[:]))
        quantise_w1(1, 0)
        v_codes[1] = successor([P, S], U32, "v_codes1", "grouped10")
        for start in range(0, S, HALF):
            nc.vector.tensor_copy(v_codes[1][:, start : start + HALF], tab[1][:].indirect(idx[:, start // 16 : (start + HALF) // 16]))

        def first_stage(b, start, count, negate_on_vector=False, after_first_pair=None):
            tiles = count // P
            bounded, negated = [], []
            for t in range(tiles):
                tokens = slice(start + t * P, start + (t + 1) * P)
                acc1 = bank([P, BANK], "acc1", "a", 2)
                acc2 = bank([P, BANK], "acc2", "b", 2)
                for a in range(2):
                    nc.tensor.matmul_mx(
                        out=acc1[:], lhsT=v_codes[a][:, tokens].bitcast(FP8X4), lhsT_scale=v_plane[4 * a : P, tokens],
                        rhs=w1_codes[a, b][:].bitcast(FP8X4), rhs_scale=w1_plane[a, b][:], start=(a == 0), stop=(a == 1),
                    )
                for a in range(2):
                    nc.tensor.matmul_mx(
                        out=acc2[:], lhsT=v_codes[a][:, tokens].bitcast(FP8X4), lhsT_scale=v_plane[4 * a : P, tokens],
                        rhs=w2_codes[a, b][:].bitcast(FP8X4), rhs_scale=w2_plane[4 * a : P, b * PASS : (b + 1) * PASS],
                        start=(a == 0), stop=(a == 1),
                    )
                tanh_t = small([P, PACK, P], F32, "tanh_t")
                neg_t = small([P, PACK, P], F32, "neg_t")
                nc.scalar.activation(tanh_t[:], acc1[:].rearrange("j (p i) -> j i p", i=PACK), ACT.Tanh, bias=zero[:])
                if negate_on_vector:
                    nc.vector.tensor_scalar_mul(neg_t[:], acc2[:].rearrange("j (p i) -> j i p", i=PACK), -1.0)
                else:
                    nc.scalar.activation(neg_t[:], acc2[:].rearrange("j (p i) -> j i p", i=PACK), ACT.Copy, scale=-1.0)
                bounded.append(tanh_t)
                negated.append(neg_t)
            for i in range(PACK):
                diff = bank([P, tiles, P], "diff", "d", 4)
                for t in range(tiles):
                    nc.tensor.matmul(diff[:, t, :], bounded[t][:, i, :], ident[:], start=True, stop=False, is_transpose=True)
                    nc.tensor.matmul(diff[:, t, :], negated[t][:, i, :], ident[:], start=False, stop=True, is_transpose=True)
                h_sb = ring.tile([P, count], F32, name="h_sb", tag="h", bufs=12, align_bytes=64)
                col = b * PACK + i
                nc.scalar.activation(h_sb[:], diff[:].rearrange("p t j -> p (t j)"), ACT.Square, scale=root[:, col : col + 1])
                entries = slice(start // 16, (start + count) // 16)
                nc.vector.tensor_tensor(pages[i][:].indirect(idx2[:, entries]), h_sb[:], wgs_sb[:, start : start + count], ALU.mult)
                if i == 1 and after_first_pair is not None:
                    after_first_pair()

        def gather(x_row, i, start, count):
            entries = slice(start // 16, (start + count) // 16)
            nc.vector.tensor_tensor(x_row, pages[i][:].indirect(idx3[:, entries]), wgt_sb[:, start : start + count], ALU.mult)

        z_codes = [held([P, M], U32, f"z_codes{b}") for b in range(2)]
        z_plane = [held([P, M], U8, f"z_plane{b}") for b in range(2)]

        def square_pace(b):
            for i in range(PACK):
                nc.scalar.activation(pace_sb[b][:, i, :], pace_sb[b][:, i, :], ACT.Square)

        def roots_by_transposes(b, pairs, x_tile, start, count, staged):
            tiles = count // P
            z_t = small([P, tiles, pairs, P, 2], BF16, "z_t")
            for u in range(pairs):
                total = bank([P, tiles, 2, P], "total", "d", 4)
                for n, source in enumerate((pace_sb[b], x_tile)):
                    for t in range(tiles):
                        for e in range(2):
                            nc.tensor.matmul(
                                total[:, t, e, :], source[:, 2 * u + e, start + t * P : start + (t + 1) * P], ident[:],
                                start=((n, t, e) == (0, 0, 0)), stop=((n, t, e) == (1, tiles - 1, 1)), is_transpose=True,
                            )
                nc.scalar.activation(z_t[:, :, u, :, :], total[:].rearrange("m t e p -> m t p e"), ACT.Sqrt)
            z_words = z_t[:].rearrange("m t u p e -> m (t u p e)").bitcast(F32)
            back = bank([P, pairs, count], "back", "b", 2)
            for t in range(tiles):
                for u in range(pairs):
                    place = pairs * t + u
                    nc.tensor.transpose(back[:, u, t * P : (t + 1) * P], z_words[:, place * P : (place + 1) * P], ident[:])
            staged_words = staged.rearrange("p m i -> p (m i)").bitcast(F32).rearrange("p (m u) -> p m u", u=2)
            nc.scalar.copy(staged_words[:, :, 0:pairs], back[:].rearrange("p u m -> p m u"))

        def quantise_z(b, start, count, staged):
            cols = slice(start, start + count)
            nc.vector.quantize_mx(
                out=z_codes[b][:, cols].bitcast(FP8X4), scales=z_plane[b][:, cols], in_=staged.rearrange("p m i -> p (m i)")
            )

        result_banks = [("d", 4)] * 4 + [("a", 2)] * 2 + [("b", 2)] * 2

        def last_product(start, count):
            for first in range(start, start + count, P):
                cols = slice(first, first + P)
                res = bank([P, N // P, P], "res", *result_banks[first // P])
                for b in range(2):
                    for nt in range(N // P):
                        nc.tensor.matmul_mx(
                            out=res[:, nt, :], lhsT=w3_codes[:, b, 2 * nt * P : 2 * (nt + 1) * P].bitcast(FP4X4),
                            lhsT_scale=w3_plane[:, b, nt * P : (nt + 1) * P],
                            rhs=z_codes[b][:, cols].bitcast(FP8X4), rhs_scale=z_plane[b][:, cols],
                            start=(b == 0 and nt == 0), stop=(b == 1 and nt == N // P - 1),
                        )
                res_sb = small([P, N // P, P], F32, "res_sb")
                if first >= M - 2 * P:
                    nc.vector.tensor_copy(res_sb[:], res[:])
                else:
                    nc.scalar.copy(res_sb[:], res[:])
                nc.sync.dma_start(out=out[:, cols].rearrange("(nt p) m -> p nt m", p=P), in_=res_sb[:])

        first_stage(0, 0, 128, negate_on_vector=True)
        first_stage(0, 128, 128, negate_on_vector=True)
        first_stage(0, 256, 256)
        first_stage(0, 512, 512)
        pace_sb = []
        for b in range(2):
            tile_b = successor([P, PACK, M], F32, f"pace{b}", f"table_then_pace{b}")
            nc.sync.dma_start(out=tile_b[:], in_=pace[b * PASS : (b + 1) * PASS, :].rearrange("(p i) m -> p i m", i=PACK))
            pace_sb.append(tile_b)
        quantise_w1(0, 1)
        quantise_w1(1, 1)
        x0 = held([P, PACK, M], F32, "x0")
        for start in range(0, M, HALF):
            for i in range(PACK):
                gather(x0[:, i, start : start + HALF], i, start, HALF)
        x1 = held([P, 2, M], F32, "x1")

        def gather_first_pair():
            for start in range(0, M, HALF):
                for i in range(2):
                    gather(x1[:, i, start : start + HALF], i, start, HALF)

        first_stage(1, 0, 512)
        first_stage(1, 512, 512, after_first_pair=gather_first_pair)
        square_pace(0)
        staged0 = successor([P, M, PACK], BF16, "staged0", "lag_a")
        for start in range(0, M, CHUNK):
            roots_by_transposes(0, 2, x0, start, CHUNK, staged0[:, start : start + CHUNK, :])
            quantise_z(0, start, CHUNK, staged0[:, start : start + CHUNK, :])
        square_pace(1)
        tapered = [(0, 256), (256, 256), (512, 256), (768, 128), (896, 128)]
        staged1 = [successor([P, count, PACK], BF16, f"staged1{c}", f"lag_{c}") for c, (start, count) in enumerate(tapered)]
        for c, (start, count) in enumerate(tapered):
            roots_by_transposes(1, 1, x1, start, count, staged1[c][:])

        def gather_and_add(x_rows, start, count):
            for e in range(2):
                gather(x_rows[:, e, :], 2 + e, start, count)
            for e in range(2):
                nc.vector.tensor_tensor(x_rows[:, e, :], x_rows[:, e, :], pace_sb[1][:, 2 + e, start : start + count], ALU.add)

        def finish(c, x_rows):
            start, count = tapered[c]
            nc.scalar.activation(staged1[c][:, :, 2:4], x_rows.rearrange("p e m -> p m e"), ACT.Sqrt)
            quantise_z(1, start, count, staged1[c][:])
            last_product(start, count)

        x_a = successor([P, 2, 2, 256], F32, "x_a", "lag_a")
        gather_and_add(x_a[:, 0], *tapered[0])
        gather_and_add(x_a[:, 1], *tapered[1])
        finish(0, x_a[:, 0])
        x_b = successor([P, 2, 256], F32, "x_b", "lag_0")
        gather_and_add(x_b[:], *tapered[2])
        finish(1, x_a[:, 1])
        x_c = successor([P, 2, 128], F32, "x_c", "lag_1")
        gather_and_add(x_c[:], *tapered[3])
        finish(2, x_b[:])
        x_d = successor([P, 2, 128], F32, "x_d", "lag_2")
        gather_and_add(x_d[:], *tapered[4])
        finish(3, x_c[:])
        finish(4, x_d[:])
